import numpy as np
import ml_dtypes


def mxq(x, axis, fmt="e4m3"):
    dtype, down = {"e4m3": (ml_dtypes.float8_e4m3fn, 7), "e5m2": (ml_dtypes.float8_e5m2, 14)}[fmt]
    v = np.moveaxis(np.asarray(x, np.float32).astype(ml_dtypes.bfloat16).astype(np.float64), axis, -1)
    blocks = v.reshape(v.shape[:-1] + (-1, 32))
    amax = np.abs(blocks).max(-1, keepdims=True)
    byte = np.maximum(np.where(amax > 0, np.frexp(amax)[1] - 1 + 127, 0) - down, 1)
    scale = np.exp2(byte - 127.0)
    codes = (blocks / scale).astype(np.float32).astype(dtype).astype(np.float64)
    return np.moveaxis((codes * scale).reshape(v.shape), -1, axis)


WIDE = False


def mx_kscale(k):
    if not WIDE:
        return np.ones(k)
    levels = np.array([10, -10, 5, -5, 0])
    if k % 512:
        return np.exp2(np.random.permutation(np.resize(levels, k // 32))).repeat(32)
    a = np.empty((k // 512, 16))
    for p in range(k // 512):
        a[p, :8] = np.random.permutation(np.resize(levels, 8))
        for g in range(8):
            far = levels[np.abs(levels - a[p, g]) >= 10]
            a[p, g + 8] = far[np.random.randint(len(far))]
    return np.exp2(a.ravel()).repeat(32)


def f64(x):
    return np.asarray(x).astype(np.float64)


def striped(idx):
    return np.tile(idx.reshape(-1, 16).T, (8, 1)).astype(np.uint16)


def unstriped(offs):
    return offs[:16].T.reshape(-1).astype(np.int64)


def striped8(idx):
    return np.concatenate([x.reshape(-1, 16).T for x in idx]).astype(np.uint16)


def runs(offs, k):
    lists = np.stack([offs[16 * r : 16 * r + 16].T.reshape(-1) for r in range(8)]).astype(np.int64)
    return lists[np.arange(k) % 512 // 64]


def pack_weight(w):
    k, n = w.shape
    w = f64(np.asarray(w, np.float32).astype(ml_dtypes.bfloat16)).reshape(k // 32, 32, n)
    amax = np.abs(w).max(1)
    byte = np.clip(np.where(amax > 0, np.frexp(amax)[1] - 1 + 127 - 7, 1), 1, 254)
    scaled = (w * np.exp2(127.0 - byte)[:, None, :]).reshape(k, n).astype(np.float32)
    words = np.ascontiguousarray(scaled.reshape(k // 512, 128, 4, n).transpose(0, 1, 3, 2)).astype(ml_dtypes.float8_e4m3fn).view(np.uint8)
    return words, np.ascontiguousarray(byte.astype(np.uint8).reshape(k // 512, 16, n))


def unpack_weight(words, scales):
    g, p, n, _ = words.shape
    vals = np.ascontiguousarray(words).view(ml_dtypes.float8_e4m3fn).astype(np.float64) * np.repeat(np.exp2(scales.astype(np.float64) - 127.0), 8, axis=1)[..., None]
    return vals.transpose(0, 1, 3, 2).reshape(g * 512, n)


E2M1 = np.array([0.0, 0.5, 1.0, 1.5, 2.0, 3.0, 4.0, 6.0, -0.0, -0.5, -1.0, -1.5, -2.0, -3.0, -4.0, -6.0])


def pack_fp4(w):
    k, n = w.shape
    w = f64(np.asarray(w, np.float32).astype(ml_dtypes.bfloat16)).reshape(k // 32, 32, n)
    amax = np.abs(w).max(1)
    mant, ex = np.frexp(amax / 6.0)
    byte = np.clip(np.where(amax > 0, np.where(mant > 0.5, ex, ex - 1) + 127, 1), 1, 254)
    scaled = (w * np.exp2(127.0 - byte)[:, None, :]).reshape(k, n).astype(np.float32)
    c = np.ascontiguousarray(scaled.reshape(k // 512, 128, 4, n).transpose(0, 1, 3, 2)).astype(ml_dtypes.float4_e2m1fn).view(np.uint8) & 0xF
    words = (c[..., 0::2] | (c[..., 1::2] << 4)).reshape(k // 512, 128, 2 * n)
    return np.ascontiguousarray(words), np.ascontiguousarray(byte.astype(np.uint8).reshape(k // 512, 16, n))


def unpack_fp4(words, scales):
    g, _, n = scales.shape
    words = np.ascontiguousarray(words).reshape(g, 128, n, 2)
    nib = np.empty((g, 128, n, 4), np.uint8)
    nib[..., 0::2] = words & 0xF
    nib[..., 1::2] = words >> 4
    vals = E2M1[nib] * np.repeat(np.exp2(scales.astype(np.float64) - 127.0), 8, axis=1)[..., None]
    return vals.transpose(0, 1, 3, 2).reshape(g * 512, n)


def sigmoid(v):
    return 1.0 / (1.0 + np.exp(-np.maximum(v, -700.0)))

def planes(y):
    n, m = y.shape
    v = y.astype(np.float32).astype(ml_dtypes.bfloat16).astype(np.float64).reshape(n // 32, 32, m)
    top = np.abs(v).max(1)
    byte = np.clip(np.where(top > 0, np.frexp(top)[1] - 1 + 127 - 7, 1), 1, 254)
    codes = (v * np.exp2(127.0 - byte)[:, None, :]).reshape(n, m).astype(np.float32).astype(ml_dtypes.float8_e4m3fn).view(np.uint8)
    words = codes.reshape(n // 512, 128, 4, m).transpose(0, 1, 3, 2)
    return np.ascontiguousarray(words), np.ascontiguousarray(byte.astype(np.uint8).reshape(n // 512, 16, m))


K, T, S, H, C = 512, 2048, 512, 512, 512


def setup_inputs():
    n = np.random.standard_normal
    s = mx_kscale(K)[:, None]
    packed_xT = pack_weight(n((K, T)) * s)
    packed_w1 = pack_fp4(n((K, H)) / np.sqrt(K) / s)
    return {
        "x_words": packed_xT[0],
        "x_scales": packed_xT[1],
        "w1_words": packed_w1[0],
        "w1_scales": packed_w1[1],
        "gs": (np.random.uniform(0.5, 1.5, (K, 1)) / s).astype(np.float32),
        "wb": (n((K, S)) / np.sqrt(K) / s).astype(np.float32),
        "offs": striped(np.random.permutation(T)[:S]),
        "n1": striped8(np.stack([np.random.permutation(S) for _ in range(8)])),
        "cand": striped(np.random.permutation(T)[:C]),
        "cb": striped(np.random.permutation(T)[:C]),
        "n2": striped8(np.stack([np.random.permutation(S) for _ in range(8)])),
        "n3": striped8(np.stack([np.random.permutation(S) for _ in range(8)])),
    }


def reference(x_words, x_scales, w1_words, w1_scales, gs, wb, offs, n1, cand, cb, n2, n3):
    x_cand = unpack_weight(x_words, x_scales)[:, unstriped(cand)]
    xq = unpack_weight(x_words, x_scales)[:, unstriped(offs)]
    y = unpack_fp4(w1_words, w1_scales).T @ xq
    z = f64(gs) * (np.maximum(y, y[np.arange(H)[:, None], runs(n1, H)]))
    a = 0.0625 * ((x_cand.T @ mxq(z, 0, "e4m3")))
    x_cb = unpack_weight(x_words, x_scales)[:, unstriped(cb)]
    b = x_cb.T @ mxq(f64(wb), 0, "e4m3")
    out_0 = a + (sigmoid(b[np.arange(C)[:, None], runs(n3, C)] - b)) * (a[np.arange(C)[:, None], runs(n2, C)] - a)
    return (out_0,) + planes(out_0)

@@ -1,0 +1,244 @@
+from contextlib import ExitStack
+
+import concourse.mybir as mybir
+from concourse.masks import make_identity
+
+F32 = mybir.dt.float32
+BF16 = mybir.dt.bfloat16
+I32 = mybir.dt.int32
+U32 = mybir.dt.uint32
+U16 = mybir.dt.uint16
+U8 = mybir.dt.uint8
+FP8X4 = mybir.dt.float8_e4m3fn_x4
+FP4X4 = mybir.dt.float4_e2m1fn_x4
+ALU = mybir.AluOpType
+ACT = mybir.ActivationFunctionType
+
+P = 128
+PACK = 4
+N = 512
+T = 2048
+HALF = 256
+FLOPS = 3 * 2 * 512 * 512 * 512
+
+
+def tile_picked_cdswpullbbig_none_po_kernel(
+    tc, x_words, x_scales, w1_words, w1_scales, gs, wb, offs, n1, cand, cb, n2, n3, out_0, out_1, out_2
+):
+    nc = tc.nc
+    with ExitStack() as ctx:
+        keep = ctx.enter_context(tc.tile_pool(name="keep", bufs=1))
+        psum = ctx.enter_context(tc.psum_pool(name="psum", bufs=1))
+
+        def sb(name, shape, dtype):
+            return keep.tile(shape, dtype, name=name, align_bytes=64)
+
+        def bank(name, tag, bufs):
+            return psum.tile([P, N], F32, name=name, tag=tag, bufs=bufs)
+
+        def load_list(name, src):
+            tile = sb(name, [P, N // 16], U16)
+            nc.sync.dma_start(tile[:], src)
+            return tile
+
+        def load_scales(tile, src, queues):
+            for q, queue in enumerate(queues):
+                queue.dma_start(tile[32 * q : 32 * q + 4, :].bitcast(I32), src[0, 4 * q : 4 * q + 4, :].bitcast(I32))
+
+        xs = sb("xs", [P, T], U8)
+        w1s_raw = sb("w1s_raw", [P, N], U8)
+        nc.vector.memset(xs[:].bitcast(I32), 0)
+        nc.vector.memset(w1s_raw[:].bitcast(I32), 0)
+        offs_t = load_list("offs_t", offs)
+        w1w_raw = sb("w1w_raw", [P, 2 * N], U8)
+        nc.scalar.dma_start(w1w_raw[:].bitcast(I32), w1_words[0].bitcast(I32))
+        cb_t = load_list("cb_t", cb)
+        load_scales(xs, x_scales, [nc.scalar] * 4)
+        xw = sb("xw", [P, T], U32)
+        nc.sync.dma_start(xw[:].bitcast(I32), x_words[0].rearrange("p n t -> p (n t)").bitcast(I32))
+        load_scales(w1s_raw, w1_scales, [nc.gpsimd, nc.gpsimd, nc.scalar, nc.scalar])
+        cand_t = load_list("cand_t", cand)
+        n1_t = load_list("n1_t", n1)
+        wb_raw = sb("wb_raw", [P, PACK, N], F32)
+        nc.sync.dma_start(wb_raw[:], wb.rearrange("(p j) c -> p j c", j=PACK))
+        gs_t = sb("gs_t", [P, PACK], F32)
+        nc.gpsimd.dma_start(gs_t[:], gs.rearrange("(p j) o -> p (j o)", j=PACK))
+        n3_t = load_list("n3_t", n3)
+        n2_t = load_list("n2_t", n2)
+
+        ident = sb("ident", [P, P], F32)
+        make_identity(nc, ident[:])
+
+        def dealt(tile):
+            return tile[:].rearrange("p (t m) -> p m t", t=PACK)
+
+        xq_s = sb("xq_s", [P, N], U8)
+        xq_w = sb("xq_w", [P, N], U32)
+        cb_s = sb("cb_s", [P, N], U8)
+        cb_w = sb("cb_w", [P, N], U32)
+        cand_s = sb("cand_s", [P, N], U8)
+        cand_w = sb("cand_w", [P, N], U32)
+        nc.vector.tensor_copy(xq_s[:], xs[:].indirect(offs_t[:]))
+        nc.vector.tensor_copy(xq_w[:], xw[:].indirect(offs_t[:]))
+
+        w1w = sb("w1w", [P, 2 * N], U8)
+        w1s = sb("w1s", [P, N], U8)
+        nc.scalar.copy(
+            w1w[:].bitcast(U16).rearrange("p (t m) -> p t m", t=PACK),
+            w1w_raw[:].bitcast(U16).rearrange("p (m t) -> p t m", t=PACK),
+        )
+        nc.gpsimd.tensor_copy(
+            w1s[:].rearrange("p (t m) -> p t m", t=PACK), w1s_raw[:].rearrange("p (m t) -> p t m", t=PACK)
+        )
+        nc.vector.tensor_copy(dealt(cb_s), xs[:].indirect(cb_t[:]))
+        nc.vector.tensor_copy(dealt(cb_w), xw[:].indirect(cb_t[:]))
+
+        def interleaved(tile):
+            return tile[:].rearrange("p (c i t) -> p c t i", i=4, t=PACK)
+
+        def by_fours(tile):
+            return tile[:].rearrange("p t (c i) -> p c t i", i=4)
+
+        wb_bf = sb("wb_bf", [P, PACK * N], BF16)
+        wb_w = sb("wb_w", [P, N], U32)
+        wb_s = sb("wb_s", [P, N], U8)
+        nc.gpsimd.tensor_scalar(interleaved(wb_bf), by_fours(wb_raw), 1.0, 0.0, ALU.mult, ALU.add)
+        nc.vector.quantize_mx(out=wb_w[:].bitcast(FP8X4), scales=wb_s[:], in_=wb_bf[:])
+
+        def cols(h):
+            return slice(HALF * h, HALF * (h + 1))
+
+        def picks(window, lst, h):
+            return window[:].indirect(lst[:, 16 * h : 16 * (h + 1)])
+
+        def gather(on_vector, out, window, lst, h):
+            if on_vector:
+                nc.vector.tensor_copy(out, picks(window, lst, h))
+            else:
+                nc.scalar.activation(out, picks(window, lst, h), ACT.Copy)
+
+        def gather_negated(on_vector, out, window, lst, h):
+            if on_vector:
+                nc.vector.tensor_scalar(out, picks(window, lst, h), -1.0, 0.0, ALU.mult, ALU.add)
+            else:
+                nc.scalar.activation(out, picks(window, lst, h), ACT.Copy, scale=-1.0)
+
+        y = []
+        for t in range(PACK):
+            acc = bank(f"y_acc{t}", "ya", 4)
+            nc.tensor.matmul_mx(
+                out=acc[:],
+                lhsT=w1w[:, 2 * P * t : 2 * P * (t + 1)].bitcast(FP4X4),
+                lhsT_scale=w1s[:, P * t : P * (t + 1)],
+                rhs=xq_w[:].bitcast(FP8X4),
+                rhs_scale=xq_s[:],
+                start=True,
+                stop=True,
+            )
+            row = sb(f"y{t}", [P, N], F32)
+            nc.scalar.copy(row[:], acc[:])
+            y.append(row)
+
+        z_w = sb("z_w", [P, N], U32)
+        z_s = sb("z_s", [P, N], U8)
+        a_acc = [bank(f"a_acc{t}", "ya", 4) for t in range(PACK)]
+        y_got = [sb(f"y_got{h}", [P, PACK, HALF], F32) for h in range(2)]
+        for h in range(2):
+            for t in range(PACK):
+                gather(False, y_got[h][:, t, :], y[t], n1_t, h)
+        nc.vector.tensor_copy(dealt(cand_s), xs[:].indirect(cand_t[:]))
+        nc.vector.tensor_copy(dealt(cand_w), xw[:].indirect(cand_t[:]))
+        for h in range(2):
+            top = sb(f"top{h}", [P, PACK, HALF], F32)
+            z_rows = sb(f"z_rows{h}", [P, PACK, HALF], BF16)
+            z_bf = sb(f"z_bf{h}", [P, PACK * HALF], BF16)
+            for t in range(PACK):
+                nc.vector.tensor_tensor(top[:, t, :], y_got[h][:, t, :], y[t][:, cols(h)], ALU.max)
+            for t in range(PACK):
+                nc.vector.tensor_scalar(z_rows[:, t, :], top[:, t, :], gs_t[:, t : t + 1], None, ALU.mult)
+            nc.vector.tensor_copy(interleaved(z_bf), by_fours(z_rows))
+            nc.vector.quantize_mx(out=z_w[:, cols(h)].bitcast(FP8X4), scales=z_s[:, cols(h)], in_=z_bf[:])
+            for t in range(PACK):
+                nc.tensor.matmul_mx(
+                    out=a_acc[t][:, cols(h)],
+                    lhsT=cand_w[:, P * t : P * (t + 1)].bitcast(FP8X4),
+                    lhsT_scale=cand_s[:, P * t : P * (t + 1)],
+                    rhs=z_w[:, cols(h)].bitcast(FP8X4),
+                    rhs_scale=z_s[:, cols(h)],
+                    start=True,
+                    stop=True,
+                )
+
+        a = []
+        for t in range(PACK):
+            row = sb(f"a{t}", [P, N], F32)
+            if t % 2 == 0:
+                nc.scalar.activation(row[:], a_acc[t][:], ACT.Copy, scale=0.0625)
+            else:
+                nc.vector.tensor_scalar(row[:], a_acc[t][:], 0.0625, None, ALU.mult)
+            a.append(row)
+        a_got = [sb(f"a_got{h}", [P, PACK, HALF], F32) for h in range(2)]
+        for h in range(2):
+            for t in range(PACK):
+                gather_negated(h == 0, a_got[h][:, t, :], a[t], n2_t, h)
+
+        def difference_turned(acc, rows, got, h, u):
+            for s in range(4):
+                t, block = 2 * u + s // 2, s % 2
+                place = acc[:, P * s : P * (s + 1)]
+                first = HALF * h + P * block
+                nc.tensor.matmul(place, rows[t][:, first : first + P], ident[:], start=True, stop=False, is_transpose=True)
+                nc.tensor.matmul(
+                    place, got[h][:, t, P * block : P * (block + 1)], ident[:], start=False, stop=True, is_transpose=True
+                )
+
+        b = []
+        for t in range(PACK):
+            acc = bank(f"b_acc{t}", "b", 2)
+            nc.tensor.matmul_mx(
+                out=acc[:],
+                lhsT=cb_w[:, P * t : P * (t + 1)].bitcast(FP8X4),
+                lhsT_scale=cb_s[:, P * t : P * (t + 1)],
+                rhs=wb_w[:].bitcast(FP8X4),
+                rhs_scale=wb_s[:],
+                start=True,
+                stop=True,
+            )
+            row = sb(f"b{t}", [P, N], F32)
+            nc.scalar.copy(row[:], acc[:])
+            b.append(row)
+        b_got = [sb(f"b_got{h}", [P, PACK, HALF], F32) for h in range(2)]
+        gate = {}
+        for h in range(2):
+            for t in range(PACK):
+                gather_negated(False, b_got[h][:, t, :], b[t], n3_t, h)
+            for u in range(2):
+                acc = bank(f"b_diff{h}{u}", "b", 2)
+                difference_turned(acc, b, b_got, h, u)
+                gate[h, u] = sb(f"gate{h}{u}", [P, N], F32)
+                nc.scalar.activation(gate[h, u][:], acc[:], ACT.Sigmoid, scale=-1.0)
+
+        out_w = sb("out_w", [P, N], U32)
+        out_s = sb("out_s", [P, N], U8)
+        out_rows = out_0.rearrange("(p t) j -> p t j", t=PACK)
+        out_words = out_1[0].rearrange("p n t -> p (n t)").bitcast(I32)
+        for h in range(2):
+            res = sb(f"res{h}", [P, PACK, HALF], F32)
+            for u in range(2):
+                acc = bank(f"a_diff{h}{u}", "ya", 4)
+                difference_turned(acc, a, a_got, h, u)
+                pull = sb(f"pull{h}{u}", [P, N], F32)
+                nc.vector.tensor_tensor(pull[:], acc[:], gate[h, u][:], ALU.mult)
+                back = bank(f"back{h}{u}", "back", 2)
+                for s in range(4):
+                    nc.tensor.transpose(back[:, P * s : P * (s + 1)], pull[:, P * s : P * (s + 1)], ident[:])
+                for s in range(2):
+                    t = 2 * u + s
+                    nc.vector.tensor_tensor(res[:, t, :], a[t][:, cols(h)], back[:, cols(s)], ALU.subtract)
+            nc.sync.dma_start(out_rows[:, :, cols(h)], res[:])
+            res_bf = sb(f"res_bf{h}", [P, PACK * HALF], BF16)
+            nc.vector.tensor_copy(interleaved(res_bf), by_fours(res))
+            nc.vector.quantize_mx(out=out_w[:, cols(h)].bitcast(FP8X4), scales=out_s[:, cols(h)], in_=res_bf[:])
+            nc.sync.dma_start(out_words[:, cols(h)], out_w[:, cols(h)].bitcast(I32))
+        for q in range(4):
+            nc.scalar.dma_start(out_2[0, 4 * q : 4 * q + 4, :].bitcast(I32), out_s[32 * q : 32 * q + 4, :].bitcast(I32))

@@ -53,16 +53,16 @@ def tile_picked_cdswpullbbig_none_po_kernel(
         w1w_raw = sb("w1w_raw", [P, 2 * N], U8)
         nc.scalar.dma_start(w1w_raw[:].bitcast(I32), w1_words[0].bitcast(I32))
         cb_t = load_list("cb_t", cb)
-        load_scales(xs, x_scales, [nc.scalar] * 4)
+        load_scales(xs, x_scales, [nc.scalar, nc.scalar, nc.sync, nc.sync])
         xw = sb("xw", [P, T], U32)
         nc.sync.dma_start(xw[:].bitcast(I32), x_words[0].rearrange("p n t -> p (n t)").bitcast(I32))
-        load_scales(w1s_raw, w1_scales, [nc.gpsimd, nc.gpsimd, nc.scalar, nc.scalar])
-        cand_t = load_list("cand_t", cand)
+        load_scales(w1s_raw, w1_scales, [nc.gpsimd, nc.gpsimd, nc.sync, nc.sync])
         n1_t = load_list("n1_t", n1)
+        cand_t = load_list("cand_t", cand)
         wb_raw = sb("wb_raw", [P, PACK, N], F32)
         nc.sync.dma_start(wb_raw[:], wb.rearrange("(p j) c -> p j c", j=PACK))
         gs_t = sb("gs_t", [P, PACK], F32)
-        nc.gpsimd.dma_start(gs_t[:], gs.rearrange("(p j) o -> p (j o)", j=PACK))
+        nc.sync.dma_start(gs_t[:], gs.rearrange("(p j) o -> p (j o)", j=PACK))
         n3_t = load_list("n3_t", n3)
         n2_t = load_list("n2_t", n2)
 
@@ -102,7 +102,9 @@ def tile_picked_cdswpullbbig_none_po_kernel(
         wb_bf = sb("wb_bf", [P, PACK * N], BF16)
         wb_w = sb("wb_w", [P, N], U32)
         wb_s = sb("wb_s", [P, N], U8)
-        nc.gpsimd.tensor_scalar(interleaved(wb_bf), by_fours(wb_raw), 1.0, 0.0, ALU.mult, ALU.add)
+        nc.gpsimd.tensor_scalar(
+            wb_bf[:].rearrange("p (c t) -> p c t", t=PACK), wb_raw[:].rearrange("p t c -> p c t"), 1.0, 0.0, ALU.mult, ALU.add
+        )
         nc.vector.quantize_mx(out=wb_w[:].bitcast(FP8X4), scales=wb_s[:], in_=wb_bf[:])
 
         def cols(h):
@@ -145,7 +147,7 @@ def tile_picked_cdswpullbbig_none_po_kernel(
         y_got = [sb(f"y_got{h}", [P, PACK, HALF], F32) for h in range(2)]
         for h in range(2):
             for t in range(PACK):
-                gather(False, y_got[h][:, t, :], y[t], n1_t, h)
+                gather(h == 0 and t >= 2, y_got[h][:, t, :], y[t], n1_t, h)
         nc.vector.tensor_copy(dealt(cand_s), xs[:].indirect(cand_t[:]))
         nc.vector.tensor_copy(dealt(cand_w), xw[:].indirect(cand_t[:]))
         for h in range(2):
@@ -169,32 +171,40 @@ def tile_picked_cdswpullbbig_none_po_kernel(
                     stop=True,
                 )
 
-        a = []
-        for t in range(PACK):
-            row = sb(f"a{t}", [P, N], F32)
-            if t % 2 == 0:
-                nc.scalar.activation(row[:], a_acc[t][:], ACT.Copy, scale=0.0625)
-            else:
-                nc.vector.tensor_scalar(row[:], a_acc[t][:], 0.0625, None, ALU.mult)
-            a.append(row)
-        a_got = [sb(f"a_got{h}", [P, PACK, HALF], F32) for h in range(2)]
-        for h in range(2):
-            for t in range(PACK):
-                gather_negated(h == 0, a_got[h][:, t, :], a[t], n2_t, h)
-
         def difference_turned(acc, rows, got, h, u):
             for s in range(4):
-                t, block = 2 * u + s // 2, s % 2
-                place = acc[:, P * s : P * (s + 1)]
-                first = HALF * h + P * block
-                nc.tensor.matmul(place, rows[t][:, first : first + P], ident[:], start=True, stop=False, is_transpose=True)
+                t, first = 2 * u + s // 2, HALF * h + P * (s % 2)
                 nc.tensor.matmul(
-                    place, got[h][:, t, P * block : P * (block + 1)], ident[:], start=False, stop=True, is_transpose=True
+                    acc[:, P * s : P * (s + 1)], rows[t][:, first : first + P], ident[:],
+                    start=(s == 0), stop=False, is_transpose=True,
+                )
+            for s in range(4):
+                t, first = 2 * u + s // 2, P * (s % 2)
+                nc.tensor.matmul(
+                    acc[:, P * s : P * (s + 1)], got[h][:, t, first : first + P], ident[:],
+                    start=False, stop=(s == 3), is_transpose=True,
                 )
 
+        out_w = sb("out_w", [P, N], U32)
+        out_s = sb("out_s", [P, N], U8)
+        out_rows = out_0.rearrange("(p t) j -> p t j", t=PACK)
+        out_words = out_1[0].rearrange("p n t -> p (n t)").bitcast(I32)
+        a = []
+        a_twin = []
+        for t in range(PACK):
+            row = sb(f"a{t}", [P, N], F32)
+            if True:
+                nc.vector.tensor_scalar(row[:], a_acc[t][:], 0.0625, None, ALU.mult)
+            else:
+                nc.scalar.activation(row[:], a_acc[t][:], ACT.Copy, scale=0.0625)
+            a.append(row)
+        a_got = [sb(f"a_got{h}", [P, PACK, HALF], F32) for h in range(2)]
+        for h in [0]:
+            for t in range(PACK):
+                gather(h == 0, a_got[h][:, t, :], a[t], n2_t, h)
         b = []
         for t in range(PACK):
-            acc = bank(f"b_acc{t}", "b", 2)
+            acc = bank(f"b_acc{t}", "b", 4)
             nc.tensor.matmul_mx(
                 out=acc[:],
                 lhsT=cb_w[:, P * t : P * (t + 1)].bitcast(FP8X4),
@@ -207,37 +217,67 @@ def tile_picked_cdswpullbbig_none_po_kernel(
             row = sb(f"b{t}", [P, N], F32)
             nc.scalar.copy(row[:], acc[:])
             b.append(row)
-        b_got = [sb(f"b_got{h}", [P, PACK, HALF], F32) for h in range(2)]
         gate = {}
-        for h in range(2):
+        b_got = {}
+        for h in [0]:
+            b_got[h] = keep.tile([P, PACK, HALF], F32, name=f"b_got{h}", tag="b_got", align_bytes=64)
             for t in range(PACK):
                 gather_negated(False, b_got[h][:, t, :], b[t], n3_t, h)
             for u in range(2):
-                acc = bank(f"b_diff{h}{u}", "b", 2)
+                acc = bank(f"b_diff{h}{u}", "ya", 4)
                 difference_turned(acc, b, b_got, h, u)
-                gate[h, u] = sb(f"gate{h}{u}", [P, N], F32)
-                nc.scalar.activation(gate[h, u][:], acc[:], ACT.Sigmoid, scale=-1.0)
-
-        out_w = sb("out_w", [P, N], U32)
-        out_s = sb("out_s", [P, N], U8)
-        out_rows = out_0.rearrange("(p t) j -> p t j", t=PACK)
-        out_words = out_1[0].rearrange("p n t -> p (n t)").bitcast(I32)
-        for h in range(2):
+                turned = sb(f"gate_turned{h}{u}", [P, N], F32)
+                nc.scalar.activation(turned[:], acc[:], ACT.Sigmoid, scale=-1.0)
+                gate[h, u] = bank(f"gate{h}{u}", "b", 4)
+                for s in range(4):
+                    nc.tensor.transpose(gate[h, u][:, P * s : P * (s + 1)], turned[:, P * s : P * (s + 1)], ident[:])
+        for h in [0]:
             res = sb(f"res{h}", [P, PACK, HALF], F32)
             for u in range(2):
-                acc = bank(f"a_diff{h}{u}", "ya", 4)
-                difference_turned(acc, a, a_got, h, u)
-                pull = sb(f"pull{h}{u}", [P, N], F32)
-                nc.vector.tensor_tensor(pull[:], acc[:], gate[h, u][:], ALU.mult)
-                back = bank(f"back{h}{u}", "back", 2)
-                for s in range(4):
-                    nc.tensor.transpose(back[:, P * s : P * (s + 1)], pull[:, P * s : P * (s + 1)], ident[:])
+                pull = sb(f"pull{h}{u}", [P, 2, HALF], F32)
+                step = sb(f"step{h}{u}", [P, 2, HALF], F32)
                 for s in range(2):
                     t = 2 * u + s
-                    nc.vector.tensor_tensor(res[:, t, :], a[t][:, cols(h)], back[:, cols(s)], ALU.subtract)
+                    nc.vector.tensor_tensor(step[:, s, :], a_got[h][:, t, :], a[t][:, cols(h)], ALU.subtract)
+                nc.vector.tensor_tensor(pull[:], gate[h, u][:].rearrange("p (s j) -> p s j", s=2), step[:], ALU.mult)
+                for s in range(2):
+                    t = 2 * u + s
+                    nc.vector.tensor_tensor(res[:, t, :], pull[:, s, :], a[t][:, cols(h)], ALU.add)
             nc.sync.dma_start(out_rows[:, :, cols(h)], res[:])
             res_bf = sb(f"res_bf{h}", [P, PACK * HALF], BF16)
-            nc.vector.tensor_copy(interleaved(res_bf), by_fours(res))
+            (nc.scalar.copy if h == 0 else nc.vector.tensor_copy)(interleaved(res_bf), by_fours(res))
+            nc.vector.quantize_mx(out=out_w[:, cols(h)].bitcast(FP8X4), scales=out_s[:, cols(h)], in_=res_bf[:])
+            nc.sync.dma_start(out_words[:, cols(h)], out_w[:, cols(h)].bitcast(I32))
+        for h in [1]:
+            b_got[h] = keep.tile([P, PACK, HALF], F32, name=f"b_got{h}", tag="b_got", align_bytes=64)
+            for t in range(PACK):
+                gather_negated(False, b_got[h][:, t, :], b[t], n3_t, h)
+            for u in range(2):
+                acc = bank(f"b_diff{h}{u}", "ya", 4)
+                difference_turned(acc, b, b_got, h, u)
+                turned = sb(f"gate_turned{h}{u}", [P, N], F32)
+                nc.scalar.activation(turned[:], acc[:], ACT.Sigmoid, scale=-1.0)
+                gate[h, u] = bank(f"gate{h}{u}", "b", 4)
+                for s in range(4):
+                    nc.tensor.transpose(gate[h, u][:, P * s : P * (s + 1)], turned[:, P * s : P * (s + 1)], ident[:])
+        for h in [1]:
+            for t in range(PACK):
+                gather(h == 0, a_got[h][:, t, :], a[t], n2_t, h)
+        for h in [1]:
+            res = sb(f"res{h}", [P, PACK, HALF], F32)
+            for u in range(2):
+                pull = sb(f"pull{h}{u}", [P, 2, HALF], F32)
+                step = sb(f"step{h}{u}", [P, 2, HALF], F32)
+                for s in range(2):
+                    t = 2 * u + s
+                    nc.vector.tensor_tensor(step[:, s, :], a_got[h][:, t, :], a[t][:, cols(h)], ALU.subtract)
+                nc.vector.tensor_tensor(pull[:], gate[h, u][:].rearrange("p (s j) -> p s j", s=2), step[:], ALU.mult)
+                for s in range(2):
+                    t = 2 * u + s
+                    nc.vector.tensor_tensor(res[:, t, :], pull[:, s, :], a[t][:, cols(h)], ALU.add)
+            nc.sync.dma_start(out_rows[:, :, cols(h)], res[:])
+            res_bf = sb(f"res_bf{h}", [P, PACK * HALF], BF16)
+            (nc.scalar.copy if h == 0 else nc.vector.tensor_copy)(interleaved(res_bf), by_fours(res))
             nc.vector.quantize_mx(out=out_w[:, cols(h)].bitcast(FP8X4), scales=out_s[:, cols(h)], in_=res_bf[:])
             nc.sync.dma_start(out_words[:, cols(h)], out_w[:, cols(h)].bitcast(I32))
         for q in range(4):

@@ -50,19 +50,17 @@ def tile_picked_cdswpullbbig_none_po_kernel(
         nc.vector.memset(xs[:].bitcast(I32), 0)
         nc.vector.memset(w1s_raw[:].bitcast(I32), 0)
         offs_t = load_list("offs_t", offs)
-        w1w_raw = sb("w1w_raw", [P, 2 * N], U8)
+        w1w_raw = keep.tile([P, 2 * N], U8, name="w1w_raw", tag="staged", align_bytes=64)
         nc.scalar.dma_start(w1w_raw[:].bitcast(I32), w1_words[0].bitcast(I32))
         cb_t = load_list("cb_t", cb)
         load_scales(xs, x_scales, [nc.scalar, nc.scalar, nc.sync, nc.sync])
         xw = sb("xw", [P, T], U32)
         nc.sync.dma_start(xw[:].bitcast(I32), x_words[0].rearrange("p n t -> p (n t)").bitcast(I32))
-        load_scales(w1s_raw, w1_scales, [nc.gpsimd, nc.gpsimd, nc.sync, nc.sync])
-        n1_t = load_list("n1_t", n1)
-        cand_t = load_list("cand_t", cand)
-        wb_raw = sb("wb_raw", [P, PACK, N], F32)
-        nc.sync.dma_start(wb_raw[:], wb.rearrange("(p j) c -> p j c", j=PACK))
+        load_scales(w1s_raw, w1_scales, [nc.sync, nc.sync, nc.sync, nc.sync])
         gs_t = sb("gs_t", [P, PACK], F32)
         nc.sync.dma_start(gs_t[:], gs.rearrange("(p j) o -> p (j o)", j=PACK))
+        n1_t = load_list("n1_t", n1)
+        cand_t = load_list("cand_t", cand)
         n3_t = load_list("n3_t", n3)
         n2_t = load_list("n2_t", n2)
 
@@ -102,6 +100,8 @@ def tile_picked_cdswpullbbig_none_po_kernel(
         wb_bf = sb("wb_bf", [P, PACK * N], BF16)
         wb_w = sb("wb_w", [P, N], U32)
         wb_s = sb("wb_s", [P, N], U8)
+        wb_raw = keep.tile([P, PACK, N], F32, name="wb_raw", tag="staged", align_bytes=64)
+        nc.scalar.dma_start(wb_raw[:], wb.rearrange("(p j) c -> p j c", j=PACK))
         nc.gpsimd.tensor_scalar(
             wb_bf[:].rearrange("p (c t) -> p c t", t=PACK), wb_raw[:].rearrange("p t c -> p c t"), 1.0, 0.0, ALU.mult, ALU.add
         )
@@ -125,6 +125,10 @@ def tile_picked_cdswpullbbig_none_po_kernel(
             else:
                 nc.scalar.activation(out, picks(window, lst, h), ACT.Copy, scale=-1.0)
 
+        gs_size = sb("gs_size", [P, PACK], F32)
+        gs_sign = sb("gs_sign", [P, PACK], F32)
+        nc.scalar.activation(gs_size[:], gs_t[:], ACT.Abs)
+        nc.scalar.activation(gs_sign[:], gs_t[:], ACT.Sign)
         y = []
         for t in range(PACK):
             acc = bank(f"y_acc{t}", "ya", 4)
@@ -138,7 +142,7 @@ def tile_picked_cdswpullbbig_none_po_kernel(
                 stop=True,
             )
             row = sb(f"y{t}", [P, N], F32)
-            nc.scalar.copy(row[:], acc[:])
+            nc.scalar.activation(row[:], acc[:], ACT.Copy, scale=gs_size[:, t : t + 1])
             y.append(row)
 
         z_w = sb("z_w", [P, N], U32)
@@ -151,13 +155,13 @@ def tile_picked_cdswpullbbig_none_po_kernel(
         nc.vector.tensor_copy(dealt(cand_s), xs[:].indirect(cand_t[:]))
         nc.vector.tensor_copy(dealt(cand_w), xw[:].indirect(cand_t[:]))
         for h in range(2):
-            top = sb(f"top{h}", [P, PACK, HALF], F32)
+            top = sb(f"top{h}", [P, PACK, HALF], BF16)
             z_rows = sb(f"z_rows{h}", [P, PACK, HALF], BF16)
             z_bf = sb(f"z_bf{h}", [P, PACK * HALF], BF16)
             for t in range(PACK):
                 nc.vector.tensor_tensor(top[:, t, :], y_got[h][:, t, :], y[t][:, cols(h)], ALU.max)
             for t in range(PACK):
-                nc.vector.tensor_scalar(z_rows[:, t, :], top[:, t, :], gs_t[:, t : t + 1], None, ALU.mult)
+                nc.vector.tensor_scalar(z_rows[:, t, :], top[:, t, :], gs_sign[:, t : t + 1], None, ALU.mult)
             nc.vector.tensor_copy(interleaved(z_bf), by_fours(z_rows))
             nc.vector.quantize_mx(out=z_w[:, cols(h)].bitcast(FP8X4), scales=z_s[:, cols(h)], in_=z_bf[:])
             for t in range(PACK):
@@ -170,6 +174,9 @@ def tile_picked_cdswpullbbig_none_po_kernel(
                     start=True,
                     stop=True,
                 )
+
+        def on_tensor(h, u):
+            return False
 
         def difference_turned(acc, rows, got, h, u):
             for s in range(4):
@@ -193,7 +200,7 @@ def tile_picked_cdswpullbbig_none_po_kernel(
         a_twin = []
         for t in range(PACK):
             row = sb(f"a{t}", [P, N], F32)
-            if True:
+            if t < 3:
                 nc.vector.tensor_scalar(row[:], a_acc[t][:], 0.0625, None, ALU.mult)
             else:
                 nc.scalar.activation(row[:], a_acc[t][:], ACT.Copy, scale=0.0625)
@@ -201,7 +208,7 @@ def tile_picked_cdswpullbbig_none_po_kernel(
         a_got = [sb(f"a_got{h}", [P, PACK, HALF], F32) for h in range(2)]
         for h in [0]:
             for t in range(PACK):
-                gather(h == 0, a_got[h][:, t, :], a[t], n2_t, h)
+                (gather_negated if on_tensor(h, t // 2) else gather)(h == 0, a_got[h][:, t, :], a[t], n2_t, h)
         b = []
         for t in range(PACK):
             acc = bank(f"b_acc{t}", "b", 4)
@@ -228,12 +235,27 @@ def tile_picked_cdswpullbbig_none_po_kernel(
                 difference_turned(acc, b, b_got, h, u)
                 turned = sb(f"gate_turned{h}{u}", [P, N], F32)
                 nc.scalar.activation(turned[:], acc[:], ACT.Sigmoid, scale=-1.0)
+                if on_tensor(h, u):
+                    gate[h, u] = turned
+                    continue
                 gate[h, u] = bank(f"gate{h}{u}", "b", 4)
                 for s in range(4):
                     nc.tensor.transpose(gate[h, u][:, P * s : P * (s + 1)], turned[:, P * s : P * (s + 1)], ident[:])
         for h in [0]:
             res = sb(f"res{h}", [P, PACK, HALF], F32)
             for u in range(2):
+                if on_tensor(h, u):
+                    acc = bank(f"a_diff{h}{u}", "ya", 4)
+                    difference_turned(acc, a, a_got, h, u)
+                    pull = sb(f"pull{h}{u}", [P, N], F32)
+                    nc.vector.tensor_tensor(pull[:], acc[:], gate[h, u][:], ALU.mult)
+                    back = bank(f"back{h}{u}", "b", 4)
+                    for s in range(4):
+                        nc.tensor.transpose(back[:, P * s : P * (s + 1)], pull[:, P * s : P * (s + 1)], ident[:])
+                    for s in range(2):
+                        t = 2 * u + s
+                        nc.vector.tensor_tensor(res[:, t, :], a[t][:, cols(h)], back[:, cols(s)], ALU.subtract)
+                    continue
                 pull = sb(f"pull{h}{u}", [P, 2, HALF], F32)
                 step = sb(f"step{h}{u}", [P, 2, HALF], F32)
                 for s in range(2):
@@ -257,15 +279,30 @@ def tile_picked_cdswpullbbig_none_po_kernel(
                 difference_turned(acc, b, b_got, h, u)
                 turned = sb(f"gate_turned{h}{u}", [P, N], F32)
                 nc.scalar.activation(turned[:], acc[:], ACT.Sigmoid, scale=-1.0)
+                if on_tensor(h, u):
+                    gate[h, u] = turned
+                    continue
                 gate[h, u] = bank(f"gate{h}{u}", "b", 4)
                 for s in range(4):
                     nc.tensor.transpose(gate[h, u][:, P * s : P * (s + 1)], turned[:, P * s : P * (s + 1)], ident[:])
         for h in [1]:
             for t in range(PACK):
-                gather(h == 0, a_got[h][:, t, :], a[t], n2_t, h)
+                (gather_negated if on_tensor(h, t // 2) else gather)(h == 0, a_got[h][:, t, :], a[t], n2_t, h)
         for h in [1]:
             res = sb(f"res{h}", [P, PACK, HALF], F32)
             for u in range(2):
+                if on_tensor(h, u):
+                    acc = bank(f"a_diff{h}{u}", "ya", 4)
+                    difference_turned(acc, a, a_got, h, u)
+                    pull = sb(f"pull{h}{u}", [P, N], F32)
+                    nc.vector.tensor_tensor(pull[:], acc[:], gate[h, u][:], ALU.mult)
+                    back = bank(f"back{h}{u}", "b", 4)
+                    for s in range(4):
+                        nc.tensor.transpose(back[:, P * s : P * (s + 1)], pull[:, P * s : P * (s + 1)], ident[:])
+                    for s in range(2):
+                        t = 2 * u + s
+                        nc.vector.tensor_tensor(res[:, t, :], a[t][:, cols(h)], back[:, cols(s)], ALU.subtract)
+                    continue
                 pull = sb(f"pull{h}{u}", [P, 2, HALF], F32)
                 step = sb(f"step{h}{u}", [P, 2, HALF], F32)
                 for s in range(2):

@@ -50,17 +50,21 @@ def tile_picked_cdswpullbbig_none_po_kernel(
         nc.vector.memset(xs[:].bitcast(I32), 0)
         nc.vector.memset(w1s_raw[:].bitcast(I32), 0)
         offs_t = load_list("offs_t", offs)
-        w1w_raw = keep.tile([P, 2 * N], U8, name="w1w_raw", tag="staged", align_bytes=64)
-        nc.scalar.dma_start(w1w_raw[:].bitcast(I32), w1_words[0].bitcast(I32))
         cb_t = load_list("cb_t", cb)
         load_scales(xs, x_scales, [nc.scalar, nc.scalar, nc.sync, nc.sync])
         xw = sb("xw", [P, T], U32)
         nc.sync.dma_start(xw[:].bitcast(I32), x_words[0].rearrange("p n t -> p (n t)").bitcast(I32))
-        load_scales(w1s_raw, w1_scales, [nc.sync, nc.sync, nc.sync, nc.sync])
+        load_scales(w1s_raw, w1_scales, [nc.scalar, nc.scalar, nc.scalar, nc.scalar])
+        w1w_raw = sb("w1w_raw", [P, 2 * N], U8)
+        nc.sync.dma_start(w1w_raw[:].bitcast(I32), w1_words[0].bitcast(I32))
+        wb_rows = wb.rearrange("(p j) c -> p j c", j=PACK)
+        wb_raw = [sb(f"wb_raw{h}", [P, PACK, HALF], F32) for h in range(2)]
+        nc.sync.dma_start(wb_raw[0][:], wb_rows[:, :, :HALF])
+        cand_t = load_list("cand_t", cand)
         gs_t = sb("gs_t", [P, PACK], F32)
         nc.sync.dma_start(gs_t[:], gs.rearrange("(p j) o -> p (j o)", j=PACK))
         n1_t = load_list("n1_t", n1)
-        cand_t = load_list("cand_t", cand)
+        nc.sync.dma_start(wb_raw[1][:], wb_rows[:, :, HALF:])
         n3_t = load_list("n3_t", n3)
         n2_t = load_list("n2_t", n2)
 
@@ -85,7 +89,7 @@ def tile_picked_cdswpullbbig_none_po_kernel(
             w1w[:].bitcast(U16).rearrange("p (t m) -> p t m", t=PACK),
             w1w_raw[:].bitcast(U16).rearrange("p (m t) -> p t m", t=PACK),
         )
-        nc.gpsimd.tensor_copy(
+        nc.vector.tensor_copy(
             w1s[:].rearrange("p (t m) -> p t m", t=PACK), w1s_raw[:].rearrange("p (m t) -> p t m", t=PACK)
         )
         nc.vector.tensor_copy(dealt(cb_s), xs[:].indirect(cb_t[:]))
@@ -97,18 +101,15 @@ def tile_picked_cdswpullbbig_none_po_kernel(
         def by_fours(tile):
             return tile[:].rearrange("p t (c i) -> p c t i", i=4)
 
-        wb_bf = sb("wb_bf", [P, PACK * N], BF16)
-        wb_w = sb("wb_w", [P, N], U32)
-        wb_s = sb("wb_s", [P, N], U8)
-        wb_raw = keep.tile([P, PACK, N], F32, name="wb_raw", tag="staged", align_bytes=64)
-        nc.scalar.dma_start(wb_raw[:], wb.rearrange("(p j) c -> p j c", j=PACK))
-        nc.gpsimd.tensor_scalar(
-            wb_bf[:].rearrange("p (c t) -> p c t", t=PACK), wb_raw[:].rearrange("p t c -> p c t"), 1.0, 0.0, ALU.mult, ALU.add
-        )
-        nc.vector.quantize_mx(out=wb_w[:].bitcast(FP8X4), scales=wb_s[:], in_=wb_bf[:])
-
         def cols(h):
             return slice(HALF * h, HALF * (h + 1))
+
+        wb_w = sb("wb_w", [P, N], U32)
+        wb_s = sb("wb_s", [P, N], U8)
+        for h in range(2):
+            wb_bf = sb(f"wb_bf{h}", [P, PACK * HALF], BF16)
+            (nc.scalar.copy if h == 0 else nc.vector.tensor_copy)(interleaved(wb_bf), by_fours(wb_raw[h]))
+            nc.vector.quantize_mx(out=wb_w[:, cols(h)].bitcast(FP8X4), scales=wb_s[:, cols(h)], in_=wb_bf[:])
 
         def picks(window, lst, h):
             return window[:].indirect(lst[:, 16 * h : 16 * (h + 1)])
@@ -151,7 +152,7 @@ def tile_picked_cdswpullbbig_none_po_kernel(
         y_got = [sb(f"y_got{h}", [P, PACK, HALF], F32) for h in range(2)]
         for h in range(2):
             for t in range(PACK):
-                gather(h == 0 and t >= 2, y_got[h][:, t, :], y[t], n1_t, h)
+                gather(h == 0 and t == 3, y_got[h][:, t, :], y[t], n1_t, h)
         nc.vector.tensor_copy(dealt(cand_s), xs[:].indirect(cand_t[:]))
         nc.vector.tensor_copy(dealt(cand_w), xw[:].indirect(cand_t[:]))
         for h in range(2):
@@ -200,7 +201,7 @@ def tile_picked_cdswpullbbig_none_po_kernel(
         a_twin = []
         for t in range(PACK):
             row = sb(f"a{t}", [P, N], F32)
-            if t < 3:
+            if True:
                 nc.vector.tensor_scalar(row[:], a_acc[t][:], 0.0625, None, ALU.mult)
             else:
                 nc.scalar.activation(row[:], a_acc[t][:], ACT.Copy, scale=0.0625)
@@ -234,7 +235,7 @@ def tile_picked_cdswpullbbig_none_po_kernel(
                 acc = bank(f"b_diff{h}{u}", "ya", 4)
                 difference_turned(acc, b, b_got, h, u)
                 turned = sb(f"gate_turned{h}{u}", [P, N], F32)
-                nc.scalar.activation(turned[:], acc[:], ACT.Sigmoid, scale=-1.0)
+                nc.scalar.activation(turned[:], acc[:], ACT.Tanh, scale=-0.5)
                 if on_tensor(h, u):
                     gate[h, u] = turned
                     continue
@@ -248,27 +249,31 @@ def tile_picked_cdswpullbbig_none_po_kernel(
                     acc = bank(f"a_diff{h}{u}", "ya", 4)
                     difference_turned(acc, a, a_got, h, u)
                     pull = sb(f"pull{h}{u}", [P, N], F32)
-                    nc.vector.tensor_tensor(pull[:], acc[:], gate[h, u][:], ALU.mult)
+                    nc.vector.scalar_tensor_tensor(pull[:], gate[h, u][:], 1.0, acc[:], ALU.add, ALU.mult)
                     back = bank(f"back{h}{u}", "b", 4)
                     for s in range(4):
                         nc.tensor.transpose(back[:, P * s : P * (s + 1)], pull[:, P * s : P * (s + 1)], ident[:])
                     for s in range(2):
                         t = 2 * u + s
-                        nc.vector.tensor_tensor(res[:, t, :], a[t][:, cols(h)], back[:, cols(s)], ALU.subtract)
+                        nc.vector.scalar_tensor_tensor(res[:, t, :], back[:, cols(s)], -0.5, a[t][:, cols(h)], ALU.mult, ALU.add)
                     continue
                 pull = sb(f"pull{h}{u}", [P, 2, HALF], F32)
                 step = sb(f"step{h}{u}", [P, 2, HALF], F32)
                 for s in range(2):
                     t = 2 * u + s
                     nc.vector.tensor_tensor(step[:, s, :], a_got[h][:, t, :], a[t][:, cols(h)], ALU.subtract)
-                nc.vector.tensor_tensor(pull[:], gate[h, u][:].rearrange("p (s j) -> p s j", s=2), step[:], ALU.mult)
+                nc.vector.scalar_tensor_tensor(pull[:], gate[h, u][:].rearrange("p (s j) -> p s j", s=2), 1.0, step[:], ALU.add, ALU.mult)
                 for s in range(2):
                     t = 2 * u + s
-                    nc.vector.tensor_tensor(res[:, t, :], pull[:, s, :], a[t][:, cols(h)], ALU.add)
-            nc.sync.dma_start(out_rows[:, :, cols(h)], res[:])
-            res_bf = sb(f"res_bf{h}", [P, PACK * HALF], BF16)
-            (nc.scalar.copy if h == 0 else nc.vector.tensor_copy)(interleaved(res_bf), by_fours(res))
-            nc.vector.quantize_mx(out=out_w[:, cols(h)].bitcast(FP8X4), scales=out_s[:, cols(h)], in_=res_bf[:])
+                    nc.vector.scalar_tensor_tensor(res[:, t, :], pull[:, s, :], 0.5, a[t][:, cols(h)], ALU.mult, ALU.add)
+                nc.sync.dma_start(out_rows[:, 2 * u : 2 * u + 2, cols(h)], res[:, 2 * u : 2 * u + 2, :])
+            for piece in range(2):
+                span = slice(HALF * h + P * piece, HALF * h + P * (piece + 1))
+                res_bf = sb(f"res_bf{h}{piece}", [P, PACK * P], BF16)
+                (nc.scalar.copy if h == 0 or piece == 0 else nc.vector.tensor_copy)(
+                    interleaved(res_bf), res[:, :, P * piece : P * (piece + 1)].rearrange("p t (c i) -> p c t i", i=4)
+                )
+                nc.vector.quantize_mx(out=out_w[:, span].bitcast(FP8X4), scales=out_s[:, span], in_=res_bf[:])
             nc.sync.dma_start(out_words[:, cols(h)], out_w[:, cols(h)].bitcast(I32))
         for h in [1]:
             b_got[h] = keep.tile([P, PACK, HALF], F32, name=f"b_got{h}", tag="b_got", align_bytes=64)
@@ -278,7 +283,7 @@ def tile_picked_cdswpullbbig_none_po_kernel(
                 acc = bank(f"b_diff{h}{u}", "ya", 4)
                 difference_turned(acc, b, b_got, h, u)
                 turned = sb(f"gate_turned{h}{u}", [P, N], F32)
-                nc.scalar.activation(turned[:], acc[:], ACT.Sigmoid, scale=-1.0)
+                nc.scalar.activation(turned[:], acc[:], ACT.Tanh, scale=-0.5)
                 if on_tensor(h, u):
                     gate[h, u] = turned
                     continue
@@ -295,27 +300,31 @@ def tile_picked_cdswpullbbig_none_po_kernel(
                     acc = bank(f"a_diff{h}{u}", "ya", 4)
                     difference_turned(acc, a, a_got, h, u)
                     pull = sb(f"pull{h}{u}", [P, N], F32)
-                    nc.vector.tensor_tensor(pull[:], acc[:], gate[h, u][:], ALU.mult)
+                    nc.vector.scalar_tensor_tensor(pull[:], gate[h, u][:], 1.0, acc[:], ALU.add, ALU.mult)
                     back = bank(f"back{h}{u}", "b", 4)
                     for s in range(4):
                         nc.tensor.transpose(back[:, P * s : P * (s + 1)], pull[:, P * s : P * (s + 1)], ident[:])
                     for s in range(2):
                         t = 2 * u + s
-                        nc.vector.tensor_tensor(res[:, t, :], a[t][:, cols(h)], back[:, cols(s)], ALU.subtract)
+                        nc.vector.scalar_tensor_tensor(res[:, t, :], back[:, cols(s)], -0.5, a[t][:, cols(h)], ALU.mult, ALU.add)
                     continue
                 pull = sb(f"pull{h}{u}", [P, 2, HALF], F32)
                 step = sb(f"step{h}{u}", [P, 2, HALF], F32)
                 for s in range(2):
                     t = 2 * u + s
                     nc.vector.tensor_tensor(step[:, s, :], a_got[h][:, t, :], a[t][:, cols(h)], ALU.subtract)
-                nc.vector.tensor_tensor(pull[:], gate[h, u][:].rearrange("p (s j) -> p s j", s=2), step[:], ALU.mult)
+                nc.vector.scalar_tensor_tensor(pull[:], gate[h, u][:].rearrange("p (s j) -> p s j", s=2), 1.0, step[:], ALU.add, ALU.mult)
                 for s in range(2):
                     t = 2 * u + s
-                    nc.vector.tensor_tensor(res[:, t, :], pull[:, s, :], a[t][:, cols(h)], ALU.add)
-            nc.sync.dma_start(out_rows[:, :, cols(h)], res[:])
-            res_bf = sb(f"res_bf{h}", [P, PACK * HALF], BF16)
-            (nc.scalar.copy if h == 0 else nc.vector.tensor_copy)(interleaved(res_bf), by_fours(res))
-            nc.vector.quantize_mx(out=out_w[:, cols(h)].bitcast(FP8X4), scales=out_s[:, cols(h)], in_=res_bf[:])
+                    nc.vector.scalar_tensor_tensor(res[:, t, :], pull[:, s, :], 0.5, a[t][:, cols(h)], ALU.mult, ALU.add)
+                nc.sync.dma_start(out_rows[:, 2 * u : 2 * u + 2, cols(h)], res[:, 2 * u : 2 * u + 2, :])
+            for piece in range(2):
+                span = slice(HALF * h + P * piece, HALF * h + P * (piece + 1))
+                res_bf = sb(f"res_bf{h}{piece}", [P, PACK * P], BF16)
+                (nc.scalar.copy if h == 0 or piece == 0 else nc.vector.tensor_copy)(
+                    interleaved(res_bf), res[:, :, P * piece : P * (piece + 1)].rearrange("p t (c i) -> p c t i", i=4)
+                )
+                nc.vector.quantize_mx(out=out_w[:, span].bitcast(FP8X4), scales=out_s[:, span], in_=res_bf[:])
             nc.sync.dma_start(out_words[:, cols(h)], out_w[:, cols(h)].bitcast(I32))
         for q in range(4):
             nc.scalar.dma_start(out_2[0, 4 * q : 4 * q + 4, :].bitcast(I32), out_s[32 * q : 32 * q + 4, :].bitcast(I32))

@@ -19,7 +19,8 @@ PACK = 4
 N = 512
 T = 2048
 HALF = 256
-FLOPS = 3 * 2 * 512 * 512 * 512
+RING = 4
+FLOPS = 3 * 2 * N * N * N
 
 
 def tile_picked_cdswpullbbig_none_po_kernel(
@@ -33,8 +34,8 @@ def tile_picked_cdswpullbbig_none_po_kernel(
         def sb(name, shape, dtype):
             return keep.tile(shape, dtype, name=name, align_bytes=64)
 
-        def bank(name, tag, bufs):
-            return psum.tile([P, N], F32, name=name, tag=tag, bufs=bufs)
+        def bank(name, ring):
+            return psum.tile([P, N], F32, name=name, tag=ring, bufs=RING)
 
         def load_list(name, src):
             tile = sb(name, [P, N // 16], U16)
@@ -45,6 +46,27 @@ def tile_picked_cdswpullbbig_none_po_kernel(
             for q, queue in enumerate(queues):
                 queue.dma_start(tile[32 * q : 32 * q + 4, :].bitcast(I32), src[0, 4 * q : 4 * q + 4, :].bitcast(I32))
 
+        def cols(h):
+            return slice(HALF * h, HALF * (h + 1))
+
+        def dealt(tile):
+            return tile[:].rearrange("p (t m) -> p m t", t=PACK)
+
+        def interleaved(tile):
+            return tile[:].rearrange("p (c i t) -> p c t i", i=4, t=PACK)
+
+        def by_fours(rows):
+            return rows.rearrange("p t (c i) -> p c t i", i=4)
+
+        def picks(window, offsets, h):
+            return window[:].indirect(offsets[:, HALF // 16 * h : HALF // 16 * (h + 1)])
+
+        def gather(on_vector, out, window, offsets, h):
+            if on_vector:
+                nc.vector.tensor_copy(out, picks(window, offsets, h))
+            else:
+                nc.scalar.activation(out, picks(window, offsets, h), ACT.Copy)
+
         xs = sb("xs", [P, T], U8)
         w1s_raw = sb("w1s_raw", [P, N], U8)
         nc.vector.memset(xs[:].bitcast(I32), 0)
@@ -54,25 +76,22 @@ def tile_picked_cdswpullbbig_none_po_kernel(
         load_scales(xs, x_scales, [nc.scalar, nc.scalar, nc.sync, nc.sync])
         xw = sb("xw", [P, T], U32)
         nc.sync.dma_start(xw[:].bitcast(I32), x_words[0].rearrange("p n t -> p (n t)").bitcast(I32))
-        load_scales(w1s_raw, w1_scales, [nc.scalar, nc.scalar, nc.scalar, nc.scalar])
+        load_scales(w1s_raw, w1_scales, [nc.scalar] * 4)
         w1w_raw = sb("w1w_raw", [P, 2 * N], U8)
         nc.sync.dma_start(w1w_raw[:].bitcast(I32), w1_words[0].bitcast(I32))
         wb_rows = wb.rearrange("(p j) c -> p j c", j=PACK)
         wb_raw = [sb(f"wb_raw{h}", [P, PACK, HALF], F32) for h in range(2)]
-        nc.sync.dma_start(wb_raw[0][:], wb_rows[:, :, :HALF])
+        nc.sync.dma_start(wb_raw[0][:], wb_rows[:, :, cols(0)])
         cand_t = load_list("cand_t", cand)
         gs_t = sb("gs_t", [P, PACK], F32)
         nc.sync.dma_start(gs_t[:], gs.rearrange("(p j) o -> p (j o)", j=PACK))
         n1_t = load_list("n1_t", n1)
-        nc.sync.dma_start(wb_raw[1][:], wb_rows[:, :, HALF:])
+        nc.sync.dma_start(wb_raw[1][:], wb_rows[:, :, cols(1)])
         n3_t = load_list("n3_t", n3)
         n2_t = load_list("n2_t", n2)
 
         ident = sb("ident", [P, P], F32)
         make_identity(nc, ident[:])
-
-        def dealt(tile):
-            return tile[:].rearrange("p (t m) -> p m t", t=PACK)
 
         xq_s = sb("xq_s", [P, N], U8)
         xq_w = sb("xq_w", [P, N], U32)
@@ -89,52 +108,35 @@ def tile_picked_cdswpullbbig_none_po_kernel(
             w1w[:].bitcast(U16).rearrange("p (t m) -> p t m", t=PACK),
             w1w_raw[:].bitcast(U16).rearrange("p (m t) -> p t m", t=PACK),
         )
-        nc.vector.tensor_copy(
+        nc.gpsimd.tensor_copy(
             w1s[:].rearrange("p (t m) -> p t m", t=PACK), w1s_raw[:].rearrange("p (m t) -> p t m", t=PACK)
         )
         nc.vector.tensor_copy(dealt(cb_s), xs[:].indirect(cb_t[:]))
         nc.vector.tensor_copy(dealt(cb_w), xw[:].indirect(cb_t[:]))
 
-        def interleaved(tile):
-            return tile[:].rearrange("p (c i t) -> p c t i", i=4, t=PACK)
-
-        def by_fours(tile):
-            return tile[:].rearrange("p t (c i) -> p c t i", i=4)
-
-        def cols(h):
-            return slice(HALF * h, HALF * (h + 1))
-
         wb_w = sb("wb_w", [P, N], U32)
         wb_s = sb("wb_s", [P, N], U8)
         for h in range(2):
             wb_bf = sb(f"wb_bf{h}", [P, PACK * HALF], BF16)
-            (nc.scalar.copy if h == 0 else nc.vector.tensor_copy)(interleaved(wb_bf), by_fours(wb_raw[h]))
+            nc.gpsimd.tensor_scalar(
+                wb_bf[:].rearrange("p (c t) -> p c t", t=PACK),
+                wb_raw[h][:].rearrange("p t c -> p c t"),
+                1.0,
+                0.0,
+                ALU.mult,
+                ALU.add,
+            )
             nc.vector.quantize_mx(out=wb_w[:, cols(h)].bitcast(FP8X4), scales=wb_s[:, cols(h)], in_=wb_bf[:])
-
-        def picks(window, lst, h):
-            return window[:].indirect(lst[:, 16 * h : 16 * (h + 1)])
-
-        def gather(on_vector, out, window, lst, h):
-            if on_vector:
-                nc.vector.tensor_copy(out, picks(window, lst, h))
-            else:
-                nc.scalar.activation(out, picks(window, lst, h), ACT.Copy)
-
-        def gather_negated(on_vector, out, window, lst, h):
-            if on_vector:
-                nc.vector.tensor_scalar(out, picks(window, lst, h), -1.0, 0.0, ALU.mult, ALU.add)
-            else:
-                nc.scalar.activation(out, picks(window, lst, h), ACT.Copy, scale=-1.0)
 
         gs_size = sb("gs_size", [P, PACK], F32)
         gs_sign = sb("gs_sign", [P, PACK], F32)
         nc.scalar.activation(gs_size[:], gs_t[:], ACT.Abs)
         nc.scalar.activation(gs_sign[:], gs_t[:], ACT.Sign)
-        y = []
+        y_sized = []
         for t in range(PACK):
-            acc = bank(f"y_acc{t}", "ya", 4)
+            y_acc = bank(f"y_acc{t}", "ya")
             nc.tensor.matmul_mx(
-                out=acc[:],
+                out=y_acc[:],
                 lhsT=w1w[:, 2 * P * t : 2 * P * (t + 1)].bitcast(FP4X4),
                 lhsT_scale=w1s[:, P * t : P * (t + 1)],
                 rhs=xq_w[:].bitcast(FP8X4),
@@ -142,17 +144,16 @@ def tile_picked_cdswpullbbig_none_po_kernel(
                 start=True,
                 stop=True,
             )
-            row = sb(f"y{t}", [P, N], F32)
-            nc.scalar.activation(row[:], acc[:], ACT.Copy, scale=gs_size[:, t : t + 1])
-            y.append(row)
+            y_sized.append(sb(f"y{t}", [P, N], F32))
+            nc.scalar.activation(y_sized[t][:], y_acc[:], ACT.Copy, scale=gs_size[:, t : t + 1])
 
         z_w = sb("z_w", [P, N], U32)
         z_s = sb("z_s", [P, N], U8)
-        a_acc = [bank(f"a_acc{t}", "ya", 4) for t in range(PACK)]
+        a_acc = [bank(f"a_acc{t}", "ya") for t in range(PACK)]
         y_got = [sb(f"y_got{h}", [P, PACK, HALF], F32) for h in range(2)]
         for h in range(2):
             for t in range(PACK):
-                gather(h == 0 and t == 3, y_got[h][:, t, :], y[t], n1_t, h)
+                gather(h == 0 and t == PACK - 1, y_got[h][:, t, :], y_sized[t], n1_t, h)
         nc.vector.tensor_copy(dealt(cand_s), xs[:].indirect(cand_t[:]))
         nc.vector.tensor_copy(dealt(cand_w), xw[:].indirect(cand_t[:]))
         for h in range(2):
@@ -160,10 +161,10 @@ def tile_picked_cdswpullbbig_none_po_kernel(
             z_rows = sb(f"z_rows{h}", [P, PACK, HALF], BF16)
             z_bf = sb(f"z_bf{h}", [P, PACK * HALF], BF16)
             for t in range(PACK):
-                nc.vector.tensor_tensor(top[:, t, :], y_got[h][:, t, :], y[t][:, cols(h)], ALU.max)
+                nc.vector.tensor_tensor(top[:, t, :], y_got[h][:, t, :], y_sized[t][:, cols(h)], ALU.max)
             for t in range(PACK):
                 nc.vector.tensor_scalar(z_rows[:, t, :], top[:, t, :], gs_sign[:, t : t + 1], None, ALU.mult)
-            nc.vector.tensor_copy(interleaved(z_bf), by_fours(z_rows))
+            nc.vector.tensor_copy(interleaved(z_bf), by_fours(z_rows[:]))
             nc.vector.quantize_mx(out=z_w[:, cols(h)].bitcast(FP8X4), scales=z_s[:, cols(h)], in_=z_bf[:])
             for t in range(PACK):
                 nc.tensor.matmul_mx(
@@ -176,45 +177,28 @@ def tile_picked_cdswpullbbig_none_po_kernel(
                     stop=True,
                 )
 
-        def on_tensor(h, u):
-            return False
-
-        def difference_turned(acc, rows, got, h, u):
-            for s in range(4):
-                t, first = 2 * u + s // 2, HALF * h + P * (s % 2)
-                nc.tensor.matmul(
-                    acc[:, P * s : P * (s + 1)], rows[t][:, first : first + P], ident[:],
-                    start=(s == 0), stop=False, is_transpose=True,
-                )
-            for s in range(4):
-                t, first = 2 * u + s // 2, P * (s % 2)
-                nc.tensor.matmul(
-                    acc[:, P * s : P * (s + 1)], got[h][:, t, first : first + P], ident[:],
-                    start=False, stop=(s == 3), is_transpose=True,
-                )
-
         out_w = sb("out_w", [P, N], U32)
         out_s = sb("out_s", [P, N], U8)
         out_rows = out_0.rearrange("(p t) j -> p t j", t=PACK)
         out_words = out_1[0].rearrange("p n t -> p (n t)").bitcast(I32)
+
         a = []
-        a_twin = []
         for t in range(PACK):
-            row = sb(f"a{t}", [P, N], F32)
-            if True:
-                nc.vector.tensor_scalar(row[:], a_acc[t][:], 0.0625, None, ALU.mult)
-            else:
-                nc.scalar.activation(row[:], a_acc[t][:], ACT.Copy, scale=0.0625)
-            a.append(row)
+            a.append(sb(f"a{t}", [P, N], F32))
+            nc.vector.tensor_scalar(a[t][:], a_acc[t][:], 0.0625, None, ALU.mult)
         a_got = [sb(f"a_got{h}", [P, PACK, HALF], F32) for h in range(2)]
-        for h in [0]:
+
+        def gather_a(h):
             for t in range(PACK):
-                (gather_negated if on_tensor(h, t // 2) else gather)(h == 0, a_got[h][:, t, :], a[t], n2_t, h)
+                gather(h == 0, a_got[h][:, t, :], a[t], n2_t, h)
+
+        gather_a(0)
+
         b = []
         for t in range(PACK):
-            acc = bank(f"b_acc{t}", "b", 4)
+            b_acc = bank(f"b_acc{t}", "b")
             nc.tensor.matmul_mx(
-                out=acc[:],
+                out=b_acc[:],
                 lhsT=cb_w[:, P * t : P * (t + 1)].bitcast(FP8X4),
                 lhsT_scale=cb_s[:, P * t : P * (t + 1)],
                 rhs=wb_w[:].bitcast(FP8X4),
@@ -222,109 +206,71 @@ def tile_picked_cdswpullbbig_none_po_kernel(
                 start=True,
                 stop=True,
             )
-            row = sb(f"b{t}", [P, N], F32)
-            nc.scalar.copy(row[:], acc[:])
-            b.append(row)
-        gate = {}
-        b_got = {}
-        for h in [0]:
-            b_got[h] = keep.tile([P, PACK, HALF], F32, name=f"b_got{h}", tag="b_got", align_bytes=64)
+            b.append(sb(f"b{t}", [P, N], F32))
+            nc.scalar.copy(b[t][:], b_acc[:])
+
+        def make_gates(h):
+            b_got = keep.tile([P, PACK, HALF], F32, name=f"b_got{h}", tag="b_got", align_bytes=64)
             for t in range(PACK):
-                gather_negated(False, b_got[h][:, t, :], b[t], n3_t, h)
+                nc.scalar.activation(b_got[:, t, :], picks(b[t], n3_t, h), ACT.Copy, scale=-1.0)
+            gates = []
             for u in range(2):
-                acc = bank(f"b_diff{h}{u}", "ya", 4)
-                difference_turned(acc, b, b_got, h, u)
-                turned = sb(f"gate_turned{h}{u}", [P, N], F32)
-                nc.scalar.activation(turned[:], acc[:], ACT.Tanh, scale=-0.5)
-                if on_tensor(h, u):
-                    gate[h, u] = turned
-                    continue
-                gate[h, u] = bank(f"gate{h}{u}", "b", 4)
+                b_diff = bank(f"b_diff{h}{u}", "ya")
                 for s in range(4):
-                    nc.tensor.transpose(gate[h, u][:, P * s : P * (s + 1)], turned[:, P * s : P * (s + 1)], ident[:])
-        for h in [0]:
+                    t, first = 2 * u + s // 2, HALF * h + P * (s % 2)
+                    nc.tensor.matmul(
+                        b_diff[:, P * s : P * (s + 1)],
+                        b[t][:, first : first + P],
+                        ident[:],
+                        start=(s == 0),
+                        stop=False,
+                        is_transpose=True,
+                    )
+                for s in range(4):
+                    t, first = 2 * u + s // 2, P * (s % 2)
+                    nc.tensor.matmul(
+                        b_diff[:, P * s : P * (s + 1)],
+                        b_got[:, t, first : first + P],
+                        ident[:],
+                        start=False,
+                        stop=(s == 3),
+                        is_transpose=True,
+                    )
+                turned = sb(f"gate_turned{h}{u}", [P, N], F32)
+                nc.scalar.activation(turned[:], b_diff[:], ACT.Tanh, scale=-0.5)
+                gates.append(bank(f"gate{h}{u}", "b"))
+                for s in range(4):
+                    nc.tensor.transpose(gates[u][:, P * s : P * (s + 1)], turned[:, P * s : P * (s + 1)], ident[:])
+            return gates
+
+        def finish(h, gates):
             res = sb(f"res{h}", [P, PACK, HALF], F32)
             for u in range(2):
-                if on_tensor(h, u):
-                    acc = bank(f"a_diff{h}{u}", "ya", 4)
-                    difference_turned(acc, a, a_got, h, u)
-                    pull = sb(f"pull{h}{u}", [P, N], F32)
-                    nc.vector.scalar_tensor_tensor(pull[:], gate[h, u][:], 1.0, acc[:], ALU.add, ALU.mult)
-                    back = bank(f"back{h}{u}", "b", 4)
-                    for s in range(4):
-                        nc.tensor.transpose(back[:, P * s : P * (s + 1)], pull[:, P * s : P * (s + 1)], ident[:])
-                    for s in range(2):
-                        t = 2 * u + s
-                        nc.vector.scalar_tensor_tensor(res[:, t, :], back[:, cols(s)], -0.5, a[t][:, cols(h)], ALU.mult, ALU.add)
-                    continue
                 pull = sb(f"pull{h}{u}", [P, 2, HALF], F32)
                 step = sb(f"step{h}{u}", [P, 2, HALF], F32)
                 for s in range(2):
                     t = 2 * u + s
                     nc.vector.tensor_tensor(step[:, s, :], a_got[h][:, t, :], a[t][:, cols(h)], ALU.subtract)
-                nc.vector.scalar_tensor_tensor(pull[:], gate[h, u][:].rearrange("p (s j) -> p s j", s=2), 1.0, step[:], ALU.add, ALU.mult)
+                nc.vector.scalar_tensor_tensor(
+                    pull[:], gates[u][:].rearrange("p (s j) -> p s j", s=2), 1.0, step[:], ALU.add, ALU.mult
+                )
                 for s in range(2):
                     t = 2 * u + s
-                    nc.vector.scalar_tensor_tensor(res[:, t, :], pull[:, s, :], 0.5, a[t][:, cols(h)], ALU.mult, ALU.add)
+                    nc.vector.scalar_tensor_tensor(
+                        res[:, t, :], pull[:, s, :], 0.5, a[t][:, cols(h)], ALU.mult, ALU.add
+                    )
                 nc.sync.dma_start(out_rows[:, 2 * u : 2 * u + 2, cols(h)], res[:, 2 * u : 2 * u + 2, :])
             for piece in range(2):
+                round_res = nc.vector.tensor_copy if (h, piece) == (1, 1) else nc.scalar.copy
                 span = slice(HALF * h + P * piece, HALF * h + P * (piece + 1))
                 res_bf = sb(f"res_bf{h}{piece}", [P, PACK * P], BF16)
-                (nc.scalar.copy if h == 0 or piece == 0 else nc.vector.tensor_copy)(
-                    interleaved(res_bf), res[:, :, P * piece : P * (piece + 1)].rearrange("p t (c i) -> p c t i", i=4)
-                )
+                round_res(interleaved(res_bf), by_fours(res[:, :, P * piece : P * (piece + 1)]))
                 nc.vector.quantize_mx(out=out_w[:, span].bitcast(FP8X4), scales=out_s[:, span], in_=res_bf[:])
             nc.sync.dma_start(out_words[:, cols(h)], out_w[:, cols(h)].bitcast(I32))
-        for h in [1]:
-            b_got[h] = keep.tile([P, PACK, HALF], F32, name=f"b_got{h}", tag="b_got", align_bytes=64)
-            for t in range(PACK):
-                gather_negated(False, b_got[h][:, t, :], b[t], n3_t, h)
-            for u in range(2):
-                acc = bank(f"b_diff{h}{u}", "ya", 4)
-                difference_turned(acc, b, b_got, h, u)
-                turned = sb(f"gate_turned{h}{u}", [P, N], F32)
-                nc.scalar.activation(turned[:], acc[:], ACT.Tanh, scale=-0.5)
-                if on_tensor(h, u):
-                    gate[h, u] = turned
-                    continue
-                gate[h, u] = bank(f"gate{h}{u}", "b", 4)
-                for s in range(4):
-                    nc.tensor.transpose(gate[h, u][:, P * s : P * (s + 1)], turned[:, P * s : P * (s + 1)], ident[:])
-        for h in [1]:
-            for t in range(PACK):
-                (gather_negated if on_tensor(h, t // 2) else gather)(h == 0, a_got[h][:, t, :], a[t], n2_t, h)
-        for h in [1]:
-            res = sb(f"res{h}", [P, PACK, HALF], F32)
-            for u in range(2):
-                if on_tensor(h, u):
-                    acc = bank(f"a_diff{h}{u}", "ya", 4)
-                    difference_turned(acc, a, a_got, h, u)
-                    pull = sb(f"pull{h}{u}", [P, N], F32)
-                    nc.vector.scalar_tensor_tensor(pull[:], gate[h, u][:], 1.0, acc[:], ALU.add, ALU.mult)
-                    back = bank(f"back{h}{u}", "b", 4)
-                    for s in range(4):
-                        nc.tensor.transpose(back[:, P * s : P * (s + 1)], pull[:, P * s : P * (s + 1)], ident[:])
-                    for s in range(2):
-                        t = 2 * u + s
-                        nc.vector.scalar_tensor_tensor(res[:, t, :], back[:, cols(s)], -0.5, a[t][:, cols(h)], ALU.mult, ALU.add)
-                    continue
-                pull = sb(f"pull{h}{u}", [P, 2, HALF], F32)
-                step = sb(f"step{h}{u}", [P, 2, HALF], F32)
-                for s in range(2):
-                    t = 2 * u + s
-                    nc.vector.tensor_tensor(step[:, s, :], a_got[h][:, t, :], a[t][:, cols(h)], ALU.subtract)
-                nc.vector.scalar_tensor_tensor(pull[:], gate[h, u][:].rearrange("p (s j) -> p s j", s=2), 1.0, step[:], ALU.add, ALU.mult)
-                for s in range(2):
-                    t = 2 * u + s
-                    nc.vector.scalar_tensor_tensor(res[:, t, :], pull[:, s, :], 0.5, a[t][:, cols(h)], ALU.mult, ALU.add)
-                nc.sync.dma_start(out_rows[:, 2 * u : 2 * u + 2, cols(h)], res[:, 2 * u : 2 * u + 2, :])
-            for piece in range(2):
-                span = slice(HALF * h + P * piece, HALF * h + P * (piece + 1))
-                res_bf = sb(f"res_bf{h}{piece}", [P, PACK * P], BF16)
-                (nc.scalar.copy if h == 0 or piece == 0 else nc.vector.tensor_copy)(
-                    interleaved(res_bf), res[:, :, P * piece : P * (piece + 1)].rearrange("p t (c i) -> p c t i", i=4)
-                )
-                nc.vector.quantize_mx(out=out_w[:, span].bitcast(FP8X4), scales=out_s[:, span], in_=res_bf[:])
-            nc.sync.dma_start(out_words[:, cols(h)], out_w[:, cols(h)].bitcast(I32))
+
+        finish(0, make_gates(0))
+        last_gates = make_gates(1)
+        gather_a(1)
+        finish(1, last_gates)
         for q in range(4):
             nc.scalar.dma_start(out_2[0, 4 * q : 4 * q + 4, :].bitcast(I32), out_s[32 * q : 32 * q + 4, :].bitcast(I32))

from contextlib import ExitStack

import concourse.mybir as mybir
from concourse.masks import make_identity

F32 = mybir.dt.float32
BF16 = mybir.dt.bfloat16
I32 = mybir.dt.int32
U32 = mybir.dt.uint32
U16 = mybir.dt.uint16
U8 = mybir.dt.uint8
FP8X4 = mybir.dt.float8_e4m3fn_x4
FP4X4 = mybir.dt.float4_e2m1fn_x4
ALU = mybir.AluOpType
ACT = mybir.ActivationFunctionType

P = 128
PACK = 4
N = 512
T = 2048
HALF = 256
RING = 4
FLOPS = 3 * 2 * N * N * N


def tile_picked_cdswpullbbig_none_po_kernel(
    tc, x_words, x_scales, w1_words, w1_scales, gs, wb, offs, n1, cand, cb, n2, n3, out_0, out_1, out_2
):
    nc = tc.nc
    with ExitStack() as ctx:
        keep = ctx.enter_context(tc.tile_pool(name="keep", bufs=1))
        psum = ctx.enter_context(tc.psum_pool(name="psum", bufs=1))

        def sb(name, shape, dtype):
            return keep.tile(shape, dtype, name=name, align_bytes=64)

        def bank(name, ring):
            return psum.tile([P, N], F32, name=name, tag=ring, bufs=RING)

        def load_list(name, src):
            tile = sb(name, [P, N // 16], U16)
            nc.sync.dma_start(tile[:], src)
            return tile

        def load_scales(tile, src, queues):
            for q, queue in enumerate(queues):
                queue.dma_start(tile[32 * q : 32 * q + 4, :].bitcast(I32), src[0, 4 * q : 4 * q + 4, :].bitcast(I32))

        def cols(h):
            return slice(HALF * h, HALF * (h + 1))

        def dealt(tile):
            return tile[:].rearrange("p (t m) -> p m t", t=PACK)

        def interleaved(tile):
            return tile[:].rearrange("p (c i t) -> p c t i", i=4, t=PACK)

        def by_fours(rows):
            return rows.rearrange("p t (c i) -> p c t i", i=4)

        def picks(window, offsets, h):
            return window[:].indirect(offsets[:, HALF // 16 * h : HALF // 16 * (h + 1)])

        def gather(on_vector, out, window, offsets, h):
            if on_vector:
                nc.vector.tensor_copy(out, picks(window, offsets, h))
            else:
                nc.scalar.activation(out, picks(window, offsets, h), ACT.Copy)

        xs = sb("xs", [P, T], U8)
        w1s_raw = sb("w1s_raw", [P, N], U8)
        nc.vector.memset(xs[:].bitcast(I32), 0)
        nc.vector.memset(w1s_raw[:].bitcast(I32), 0)
        offs_t = load_list("offs_t", offs)
        cb_t = load_list("cb_t", cb)
        load_scales(xs, x_scales, [nc.scalar, nc.scalar, nc.sync, nc.sync])
        xw = sb("xw", [P, T], U32)
        nc.sync.dma_start(xw[:].bitcast(I32), x_words[0].rearrange("p n t -> p (n t)").bitcast(I32))
        load_scales(w1s_raw, w1_scales, [nc.scalar] * 4)
        w1w_raw = sb("w1w_raw", [P, 2 * N], U8)
        nc.sync.dma_start(w1w_raw[:].bitcast(I32), w1_words[0].bitcast(I32))
        wb_rows = wb.rearrange("(p j) c -> p j c", j=PACK)
        wb_raw = [sb(f"wb_raw{h}", [P, PACK, HALF], F32) for h in range(2)]
        nc.sync.dma_start(wb_raw[0][:], wb_rows[:, :, cols(0)])
        cand_t = load_list("cand_t", cand)
        gs_t = sb("gs_t", [P, PACK], F32)
        nc.sync.dma_start(gs_t[:], gs.rearrange("(p j) o -> p (j o)", j=PACK))
        n1_t = load_list("n1_t", n1)
        nc.sync.dma_start(wb_raw[1][:], wb_rows[:, :, cols(1)])
        n3_t = load_list("n3_t", n3)
        n2_t = load_list("n2_t", n2)

        ident = sb("ident", [P, P], F32)
        make_identity(nc, ident[:])

        xq_s = sb("xq_s", [P, N], U8)
        xq_w = sb("xq_w", [P, N], U32)
        cb_s = sb("cb_s", [P, N], U8)
        cb_w = sb("cb_w", [P, N], U32)
        cand_s = sb("cand_s", [P, N], U8)
        cand_w = sb("cand_w", [P, N], U32)
        nc.vector.tensor_copy(xq_s[:], xs[:].indirect(offs_t[:]))
        nc.vector.tensor_copy(xq_w[:], xw[:].indirect(offs_t[:]))

        w1w = sb("w1w", [P, 2 * N], U8)
        w1s = sb("w1s", [P, N], U8)
        nc.scalar.copy(
            w1w[:].bitcast(U16).rearrange("p (t m) -> p t m", t=PACK),
            w1w_raw[:].bitcast(U16).rearrange("p (m t) -> p t m", t=PACK),
        )
        nc.gpsimd.tensor_copy(
            w1s[:].rearrange("p (t m) -> p t m", t=PACK), w1s_raw[:].rearrange("p (m t) -> p t m", t=PACK)
        )
        nc.vector.tensor_copy(dealt(cb_s), xs[:].indirect(cb_t[:]))
        nc.vector.tensor_copy(dealt(cb_w), xw[:].indirect(cb_t[:]))

        wb_w = sb("wb_w", [P, N], U32)
        wb_s = sb("wb_s", [P, N], U8)
        for h in range(2):
            wb_bf = sb(f"wb_bf{h}", [P, PACK * HALF], BF16)
            nc.gpsimd.tensor_scalar(
                wb_bf[:].rearrange("p (c t) -> p c t", t=PACK),
                wb_raw[h][:].rearrange("p t c -> p c t"),
                1.0,
                0.0,
                ALU.mult,
                ALU.add,
            )
            nc.vector.quantize_mx(out=wb_w[:, cols(h)].bitcast(FP8X4), scales=wb_s[:, cols(h)], in_=wb_bf[:])

        gs_size = sb("gs_size", [P, PACK], F32)
        gs_sign = sb("gs_sign", [P, PACK], F32)
        nc.scalar.activation(gs_size[:], gs_t[:], ACT.Abs)
        nc.scalar.activation(gs_sign[:], gs_t[:], ACT.Sign)
        y_sized = []
        for t in range(PACK):
            y_acc = bank(f"y_acc{t}", "ya")
            nc.tensor.matmul_mx(
                out=y_acc[:],
                lhsT=w1w[:, 2 * P * t : 2 * P * (t + 1)].bitcast(FP4X4),
                lhsT_scale=w1s[:, P * t : P * (t + 1)],
                rhs=xq_w[:].bitcast(FP8X4),
                rhs_scale=xq_s[:],
                start=True,
                stop=True,
            )
            y_sized.append(sb(f"y{t}", [P, N], F32))
            nc.scalar.activation(y_sized[t][:], y_acc[:], ACT.Copy, scale=gs_size[:, t : t + 1])

        z_w = sb("z_w", [P, N], U32)
        z_s = sb("z_s", [P, N], U8)
        a_acc = [bank(f"a_acc{t}", "ya") for t in range(PACK)]
        y_got = [sb(f"y_got{h}", [P, PACK, HALF], F32) for h in range(2)]
        for h in range(2):
            for t in range(PACK):
                gather(h == 0 and t == PACK - 1, y_got[h][:, t, :], y_sized[t], n1_t, h)
        nc.vector.tensor_copy(dealt(cand_s), xs[:].indirect(cand_t[:]))
        nc.vector.tensor_copy(dealt(cand_w), xw[:].indirect(cand_t[:]))
        for h in range(2):
            top = sb(f"top{h}", [P, PACK, HALF], BF16)
            z_rows = sb(f"z_rows{h}", [P, PACK, HALF], BF16)
            z_bf = sb(f"z_bf{h}", [P, PACK * HALF], BF16)
            for t in range(PACK):
                nc.vector.tensor_tensor(top[:, t, :], y_got[h][:, t, :], y_sized[t][:, cols(h)], ALU.max)
            for t in range(PACK):
                nc.vector.tensor_scalar(z_rows[:, t, :], top[:, t, :], gs_sign[:, t : t + 1], None, ALU.mult)
            nc.vector.tensor_copy(interleaved(z_bf), by_fours(z_rows[:]))
            nc.vector.quantize_mx(out=z_w[:, cols(h)].bitcast(FP8X4), scales=z_s[:, cols(h)], in_=z_bf[:])
            for t in range(PACK):
                nc.tensor.matmul_mx(
                    out=a_acc[t][:, cols(h)],
                    lhsT=cand_w[:, P * t : P * (t + 1)].bitcast(FP8X4),
                    lhsT_scale=cand_s[:, P * t : P * (t + 1)],
                    rhs=z_w[:, cols(h)].bitcast(FP8X4),
                    rhs_scale=z_s[:, cols(h)],
                    start=True,
                    stop=True,
                )

        out_w = sb("out_w", [P, N], U32)
        out_s = sb("out_s", [P, N], U8)
        out_rows = out_0.rearrange("(p t) j -> p t j", t=PACK)
        out_words = out_1[0].rearrange("p n t -> p (n t)").bitcast(I32)

        a = []
        for t in range(PACK):
            a.append(sb(f"a{t}", [P, N], F32))
            nc.vector.tensor_scalar(a[t][:], a_acc[t][:], 0.0625, None, ALU.mult)
        a_got = [sb(f"a_got{h}", [P, PACK, HALF], F32) for h in range(2)]

        def gather_a(h):
            for t in range(PACK):
                gather(h == 0, a_got[h][:, t, :], a[t], n2_t, h)

        gather_a(0)

        b = []
        for t in range(PACK):
            b_acc = bank(f"b_acc{t}", "b")
            nc.tensor.matmul_mx(
                out=b_acc[:],
                lhsT=cb_w[:, P * t : P * (t + 1)].bitcast(FP8X4),
                lhsT_scale=cb_s[:, P * t : P * (t + 1)],
                rhs=wb_w[:].bitcast(FP8X4),
                rhs_scale=wb_s[:],
                start=True,
                stop=True,
            )
            b.append(sb(f"b{t}", [P, N], F32))
            nc.scalar.copy(b[t][:], b_acc[:])

        def make_gates(h):
            b_got = keep.tile([P, PACK, HALF], F32, name=f"b_got{h}", tag="b_got", align_bytes=64)
            for t in range(PACK):
                nc.scalar.activation(b_got[:, t, :], picks(b[t], n3_t, h), ACT.Copy, scale=-1.0)
            gates = []
            for u in range(2):
                b_diff = bank(f"b_diff{h}{u}", "ya")
                for s in range(4):
                    t, first = 2 * u + s // 2, HALF * h + P * (s % 2)
                    nc.tensor.matmul(
                        b_diff[:, P * s : P * (s + 1)],
                        b[t][:, first : first + P],
                        ident[:],
                        start=(s == 0),
                        stop=False,
                        is_transpose=True,
                    )
                for s in range(4):
                    t, first = 2 * u + s // 2, P * (s % 2)
                    nc.tensor.matmul(
                        b_diff[:, P * s : P * (s + 1)],
                        b_got[:, t, first : first + P],
                        ident[:],
                        start=False,
                        stop=(s == 3),
                        is_transpose=True,
                    )
                turned = sb(f"gate_turned{h}{u}", [P, N], F32)
                nc.scalar.activation(turned[:], b_diff[:], ACT.Tanh, scale=-0.5)
                gates.append(bank(f"gate{h}{u}", "b"))
                for s in range(4):
                    nc.tensor.transpose(gates[u][:, P * s : P * (s + 1)], turned[:, P * s : P * (s + 1)], ident[:])
            return gates

        def finish(h, gates):
            res = sb(f"res{h}", [P, PACK, HALF], F32)
            for u in range(2):
                pull = sb(f"pull{h}{u}", [P, 2, HALF], F32)
                step = sb(f"step{h}{u}", [P, 2, HALF], F32)
                for s in range(2):
                    t = 2 * u + s
                    nc.vector.tensor_tensor(step[:, s, :], a_got[h][:, t, :], a[t][:, cols(h)], ALU.subtract)
                nc.vector.scalar_tensor_tensor(
                    pull[:], gates[u][:].rearrange("p (s j) -> p s j", s=2), 1.0, step[:], ALU.add, ALU.mult
                )
                for s in range(2):
                    t = 2 * u + s
                    nc.vector.scalar_tensor_tensor(
                        res[:, t, :], pull[:, s, :], 0.5, a[t][:, cols(h)], ALU.mult, ALU.add
                    )
                nc.sync.dma_start(out_rows[:, 2 * u : 2 * u + 2, cols(h)], res[:, 2 * u : 2 * u + 2, :])
            for piece in range(2):
                round_res = nc.vector.tensor_copy if (h, piece) == (1, 1) else nc.scalar.copy
                span = slice(HALF * h + P * piece, HALF * h + P * (piece + 1))
                res_bf = sb(f"res_bf{h}{piece}", [P, PACK * P], BF16)
                round_res(interleaved(res_bf), by_fours(res[:, :, P * piece : P * (piece + 1)]))
                nc.vector.quantize_mx(out=out_w[:, span].bitcast(FP8X4), scales=out_s[:, span], in_=res_bf[:])
            nc.sync.dma_start(out_words[:, cols(h)], out_w[:, cols(h)].bitcast(I32))

        finish(0, make_gates(0))
        last_gates = make_gates(1)
        gather_a(1)
        finish(1, last_gates)
        for q in range(4):
            nc.scalar.dma_start(out_2[0, 4 * q : 4 * q + 4, :].bitcast(I32), out_s[32 * q : 32 * q + 4, :].bitcast(I32))
